import numpy as np, ml_dtypes
CORES = [113,118,241,246]
N = 4
T, SQ = 8192, 4096
def entries(a): return a.T.reshape(-1)
def pack(v, P): return np.ascontiguousarray(np.asarray(v, np.int32).reshape(-1, P).T)
def lists(rng, how):
    d = np.concatenate([[0], rng.integers(1 - SQ // 2, SQ // 2, N - 1), [int(rng.integers(1 - SQ // 2, 1))]])
    if how == "lag": d[1:] = -SQ
    if how == "lead": d[1:N] = SQ; d[N] = 0
    if how == "runs": m = int(rng.integers(1, N - 2)); d[m] = -abs(d[m]); d[m + 1] = d[m] + SQ; d[m + 2] = d[m]
    if how == "skew": t = int(rng.integers(2, N - 1)); d[1:] = rng.integers(SQ // 2 + 1, SQ - 1, N); d[t + 1:] *= -1; d[t] = d[t - 1] + d[t + 1]
    n = SQ + np.diff(d)
    F = np.zeros((N, T), np.int64)
    for r in range(N):
        o = rng.permutation(T)
        if how == "runs": o = (T // 16 * rng.permutation(16)[:, None] + np.arange(T // 16)).reshape(-1)
        if how == "skew": o = np.concatenate([[0, T - 1], 1 + rng.permutation(T - 2)])
        F[r, o[:n[r]]] = 1
    return {"fl": np.stack([pack(f, 16) for f in F])}
def setup_inputs(rng):
    return dict({"x": rng.standard_normal((N, 128, T), dtype=np.float32).astype(ml_dtypes.bfloat16), "st": rng.standard_normal((N, 128, SQ), dtype=np.float32).astype(ml_dtypes.bfloat16)}, **lists(rng, "uniform"))
def setup_inputs_lag(rng):
    d = setup_inputs(rng); d.update(lists(rng, "lag"))
    for k in ("x", "st"): d[k] = (d[k].astype(np.float32) * 1048576.0).astype(d[k].dtype)
    return d
def setup_inputs_lead(rng):
    d = setup_inputs(rng); d.update(lists(rng, "lead"))
    for k in ("x", "st"): d[k] = (d[k].astype(np.float32) * (1 / 1024.0)).astype(d[k].dtype)
    return d
def setup_inputs_runs(rng):
    d = setup_inputs(rng); d.update(lists(rng, "runs"))
    return d
def setup_inputs_skew(rng):
    d = setup_inputs(rng); d.update(lists(rng, "skew"))
    return d
def check_inputs(x):
    bad = []
    if x["fl"].min() < 0 or x["fl"].max() >= 2: bad.append("fl out of range")
    if int(x["fl"].sum()) > N * SQ: bad.append("more flags than the stream has columns")
    c = np.concatenate([[0], np.cumsum([int(a.sum()) for a in x["fl"]])])
    if any(c[r] < (r - 1) * SQ or c[r + 1] > (r + 2) * SQ for r in range(N)): bad.append("a rank's share of the stream reaches beyond its neighbours' parts")
    return bad
def reference(x, st, fl):
    S = np.concatenate(list(st), axis=1); X = np.concatenate(list(x), axis=1)
    F = np.concatenate([entries(f) for f in fl]) > 0; c = np.cumsum(F) - F
    Y = np.where(F[None, :], S[:, np.minimum(c, N * SQ - 1)], X)
    return {"y": np.stack([Y[:, T * r:T * r + T] for r in range(N)])}

@@ -1,0 +1,239 @@
+from concourse.bass import DstId, RemoteDMATransfer
+from concourse.mybir import dt, AluOpType as Op, AxisListType, ActivationFunctionType as Act
+
+NR, W, SQ = 4, 8192, 4096
+HALF = W // 2
+ST_CUTS = [0, 1024, 4096]
+X_CUTS = [0, 2048, 8192]
+G_CUTS = [0, 1024, 2048, 3072, 4096]
+NG = len(G_CUTS) - 1
+NS = len(ST_CUTS) - 1
+
+SCRATCH = {
+    "win": ("sbuf", [128, W + 3 * SQ], "bfloat16"),
+    "yb": ("sbuf", [128, W], "bfloat16"),
+    "fls": ("sbuf", [16, 512], "int32"),
+    "fb": ("sbuf", [16, 512], "bfloat16"),
+    "rs": ("sbuf", [16, 512], "float16"),
+    "m16": ("sbuf", [16, 128], "float32"),
+    "sel": ("sbuf", [16, 128], "bfloat16"),
+    "tri": ("sbuf", [16, 128], "bfloat16"),
+    "one": ("sbuf", [16, 128], "bfloat16"),
+    "pidx": ("sbuf", [128, 8], "int32"),
+    "pand": ("sbuf", [128, 8], "int32"),
+    "acol": ("sbuf", [128, 8], "float32"),
+    "c16": ("sbuf", [128, 512], "float32"),
+    "j1": ("sbuf", [128, 512], "float32"),
+    "dd": ("sbuf", [128, 512], "float32"),
+    "de": ("sbuf", [128, 512], "float32"),
+    "qq": ("sbuf", [128, 512], "float32"),
+    "t2": ("sbuf", [128, 512], "float32"),
+    "off": ("sbuf", [128, 512], "uint16"),
+    "cin": ("sbuf", [128, 64 * (NR - 1)], "int32"),
+    "cf": ("sbuf", [128, 64 * (NR - 1)], "float32"),
+    "cs": ("sbuf", [128, 8], "float32"),
+    "onef": ("sbuf", [128, 128], "float32"),
+    "b16": ("sbuf", [128, 8], "float32"),
+    "psF": ("psum", [128, 512], "float32"),
+    "psP": ("psum", [128, 512], "float32"),
+    "psT": ("psum", [128, 512], "float32"),
+    "psC": ("psum", [128, 512], "float32"),
+    "fo": ("dram", [128, 64], "int32"),
+    "fin": ("dram", [NR - 1, 128, 64], "int32"),
+}
+SEMAPHORES = (["fo", "fl", "fa", "ci", "xl", "go", "aL", "aR", "sent", "yst", "ysl", "k_pid", "k_m16"]
+              + ["st%d" % k for k in range(NS)]
+              + ["v%d" % k for k in range(24)] + ["t_l", "t_c"]
+              + ["vg%d" % k for k in range(NG)] + ["sg%d" % k for k in range(NG)])
+
+
+def own_col(r):
+    return W + (SQ if r > 0 else 0)
+
+
+def land_col(src, dst):
+    return own_col(dst) + SQ * (src - dst)
+
+
+def engines(mask):
+    return bin(mask).count("1")
+
+
+def masks(core, dsts, topo):
+    off = 0
+    for d in dsts:
+        if topo.same_plane(core, d):
+            off |= topo.mask(core, d)
+    out = {}
+    for d in dsts:
+        m = topo.mask(core, d)
+        out[d] = m if topo.same_plane(core, d) else m & ~off
+    return out
+
+
+def send(g, core, topo, groups, local_sem):
+    tr = []
+    n = 0
+    for dsts, mask, src, dst, rsem in groups:
+        ids = []
+        for d in dsts:
+            rid, pid = topo.addr(d, core)
+            ids.append(DstId(rid=rid, pnc=pid))
+        tr.append(RemoteDMATransfer(dst_ids=ids, dma_engine_mask=mask, remote_sem=rsem, srcs=[src],
+                                    dsts=[dst] * len(ids), alu_op=0))
+        n += engines(mask)
+    g.remote_dma_fused(tr, local_sem=local_sem)
+    return n
+
+
+def rank_program(g, core, T, topo):
+    r = T.rank_of(core)
+    if r is None:
+        return
+    S = T.sem
+    cores = list(T.cores)
+    V, A, E, Y = g.vector, g.scalar, g.tensor, g.sync
+    own = own_col(r)
+    ncols = own + SQ + (SQ if r < NR - 1 else 0)
+
+    def flag_groups(s):
+        later = list(range(s + 1, NR))
+        mk = masks(cores[s], [cores[d] for d in later], topo)
+        by = {}
+        for d in later:
+            by.setdefault(mk[cores[d]], []).append(d)
+        return sorted((m, ds) for m, ds in by.items())
+
+    def near(s):
+        return [d for d in (s + 1, s - 1) if 0 <= d < NR]
+
+    def bulk_mask(s, d):
+        return masks(cores[s], [cores[q] for q in near(s)], topo)[cores[d]]
+
+    for k in range(NS):
+        a, b = ST_CUTS[k], ST_CUTS[k + 1]
+        Y.dma_start(T.win[:, own + a:own + b], T.st[:, a:b]).then_inc(S["st%d" % k], 16)
+    Y.dma_start(T.win[:, X_CUTS[0]:X_CUTS[1]], T.x[:, X_CUTS[0]:X_CUTS[1]]).then_inc(S.xl, 16)
+    if r < NR - 1:
+        A.dma_start(T.fo[:], T.fl[:]).then_inc(S.fo, 16)
+    A.dma_start(T.fls[:], T.fl[:]).then_inc(S.fl, 16)
+
+    g.iota(T.pidx[:, 0:1], [[1, 1]], 0, 1).then_inc(S.k_pid, 1)
+    g.iota(T.m16[:], [[0, 8], [1, 16]], 0, -1, allow_small_or_imprecise_dtypes=True).then_inc(S.k_m16, 1)
+    sent = 0
+    if r < NR - 1:
+        g.wait_ge(S.fo, 16)
+        sent += send(g, core, topo, [([cores[d] for d in ds], m, T.fo[:], T.fin[r], S.fa)
+                                     for m, ds in flag_groups(r)], S.sent)
+    for k in range(NS):
+        a, b = ST_CUTS[k], ST_CUTS[k + 1]
+        g.wait_ge(S["st%d" % k], 16)
+        gr = []
+        for d in near(r):
+            lc = land_col(r, d)
+            gr.append(([cores[d]], bulk_mask(r, d), T.win[:, own + a:own + b], T.win[:, lc + a:lc + b],
+                       S.aL if d > r else S.aR))
+        sent += send(g, core, topo, gr, S.sent)
+    g.sem_inc(S.go, 1)
+
+    Y.wait_ge(S.go, 1)
+    for a, b in zip(X_CUTS[1:-1], X_CUTS[2:]):
+        Y.dma_start(T.win[:, a:b], T.x[:, a:b]).then_inc(S.xl, 16)
+
+    fa = 0
+    for s in range(r):
+        for m, ds in flag_groups(s):
+            if r in ds:
+                fa += engines(m)
+    if r > 0:
+        A.wait_ge(S.fa, fa)
+        A.dma_start(T.cin[:, 0:64 * r], T.fin[0:r]).then_inc(S.ci, 16)
+
+    cnt = [0]
+
+    def inc(ins):
+        name = "v%d" % cnt[0]
+        cnt[0] += 1
+        ins.then_inc(S[name], 1)
+        return S[name]
+
+    s_one = inc(V.memset(T.one[:], 1.0))
+    s_c16 = inc(V.memset(T.c16[:], 16.0))
+    s_onef = inc(V.memset(T.onef[:], 1.0)) if r > 0 else None
+    V.wait_ge(S.k_pid, 1)
+    s = inc(V.tensor_scalar(T.pand[:, 0:1], T.pidx[:, 0:1], 15, None, Op.bitwise_and))
+    V.wait_ge(S.k_m16, 1)
+    s_sel = inc(V.tensor_scalar(T.sel[:], T.m16[:], 0.0, None, Op.is_equal))
+    s_tri = inc(V.tensor_scalar(T.tri[:], T.m16[:], 0.0, -1.0, Op.is_le, Op.mult))
+    V.wait_ge(s, 1)
+    s = inc(V.tensor_copy(T.acol[:, 0:1], T.pand[:, 0:1]))
+    V.wait_ge(s, 1)
+    V.wait_ge(s_c16, 1)
+    s_j1 = inc(V.tensor_tensor_scan(T.j1[:], T.c16[:], T.c16[:], T.acol[:, 0:1], Op.add, Op.max))
+    V.wait_ge(S.fl, 16)
+    s_fb = inc(V.tensor_copy(T.fb[:], T.fls[:]))
+    V.wait_ge(s_fb, 1)
+    s_rs = inc(V.tensor_tensor_scan(T.rs[:], T.fb[:], T.fb[:], 0.0, Op.add, Op.max))
+
+    for q in (s_sel, s_fb, s_one, s_rs, s_tri):
+        E.wait_ge(q, 1)
+    E.matmul(T.psF[:], T.sel[:], T.fb[:], True, True)
+    E.matmul(T.psP[:], T.one[:], T.rs[:], True, False)
+    E.matmul(T.psP[:], T.tri[:], T.fb[:], False, True).then_inc(S.t_l, 1)
+
+    V.wait_ge(S.t_l, 1)
+    V.wait_ge(s_j1, 1)
+    s = inc(V.tensor_tensor(T.dd[:], T.psP[:], T.j1[:], Op.subtract))
+    V.wait_ge(s, 1)
+    s = inc(V.tensor_tensor(T.de[:], T.dd[:], T.psF[:], Op.mult))
+    V.wait_ge(s, 1)
+    s_q = inc(V.tensor_tensor(T.qq[:], T.de[:], T.j1[:], Op.add))
+
+    base = float(W - SQ * max(r - 1, 0) + 16)
+    if r > 0:
+        V.wait_ge(S.ci, 16)
+        s = inc(V.tensor_copy(T.cf[:, 0:64 * r], T.cin[:, 0:64 * r]))
+        V.wait_ge(s, 1)
+        s = inc(V.tensor_reduce(T.cs[:, 0:1], T.cf[:, 0:64 * r], AxisListType.X, Op.add))
+        E.wait_ge(s, 1)
+        E.wait_ge(s_onef, 1)
+        E.matmul(T.psC[:, 0:1], T.onef[:], T.cs[:, 0:1], True, True).then_inc(S.t_c, 1)
+        V.wait_ge(S.t_c, 1)
+        s = inc(V.tensor_scalar(T.b16[:, 0:1], T.psC[:, 0:1], base, None, Op.add))
+        V.wait_ge(s, 1)
+        base = T.b16[:, 0:1]
+    s = inc(V.tensor_scalar(T.psT[:], T.psF[:], base, None, Op.mult))
+    V.wait_ge(s, 1)
+    V.wait_ge(s_q, 1)
+    s = inc(V.tensor_tensor(T.t2[:], T.psT[:], T.qq[:], Op.add))
+    V.wait_ge(s, 1)
+    s_off = inc(V.tensor_scalar(T.off[:], T.t2[:], 16.0, None, Op.subtract))
+
+    for q in (V, A):
+        q.wait_ge(s_off, 1)
+        q.wait_ge(S.xl, 16 * (len(X_CUTS) - 1))
+        for k in range(NS):
+            q.wait_ge(S["st%d" % k], 16)
+        for d in near(r):
+            q.wait_ge(S.aR if d > r else S.aL, NS * engines(bulk_mask(d, r)))
+    for k in range(NG):
+        a, b = G_CUTS[k], G_CUTS[k + 1]
+        V.tensor_copy(T.yb[:, a:b], T.win[:, 0:ncols].indirect(T.off[:, a // 16:b // 16])).then_inc(S["vg%d" % k], 1)
+        a, b = a + HALF, b + HALF
+        A.activation(T.yb[:, a:b], T.win[:, 0:ncols].indirect(T.off[:, a // 16:b // 16]),
+                     Act.Copy).then_inc(S["sg%d" % k], 1)
+
+    for k in range(NG):
+        a, b = G_CUTS[k], G_CUTS[k + 1]
+        Y.wait_ge(S["vg%d" % k], 1)
+        Y.dma_start(T.y[:, a:b], T.yb[:, a:b]).then_inc(S.yst, 16)
+        a, b = a + HALF, b + HALF
+        if k < NG - 1:
+            Y.wait_ge(S["sg%d" % k], 1)
+            Y.dma_start(T.y[:, a:b], T.yb[:, a:b]).then_inc(S.yst, 16)
+        else:
+            A.wait_ge(S["sg%d" % k], 1)
+            A.dma_start(T.y[:, a:b], T.yb[:, a:b]).then_inc(S.ysl, 16)
+    Y.wait_ge(S.yst, 16 * (2 * NG - 1))
+    A.wait_ge(S.ysl, 16)
+    g.wait_ge(S.sent, sent)

@@ -3,11 +3,10 @@ from concourse.mybir import dt, AluOpType as Op, AxisListType, ActivationFunctio
 
 NR, W, SQ = 4, 8192, 4096
 HALF = W // 2
-ST_CUTS = [0, 1024, 4096]
-X_CUTS = [0, 2048, 8192]
-G_CUTS = [0, 1024, 2048, 3072, 4096]
-NG = len(G_CUTS) - 1
-NS = len(ST_CUTS) - 1
+RELAY = 1024
+X_CUTS = [0, 6144, 8192]
+V_CUTS = [0, 1024, 2048, 3072, 4096]
+NG = len(V_CUTS) - 1
 
 SCRATCH = {
     "win": ("sbuf", [128, W + 3 * SQ], "bfloat16"),
@@ -24,6 +23,7 @@ SCRATCH = {
     "acol": ("sbuf", [128, 8], "float32"),
     "c16": ("sbuf", [128, 512], "float32"),
     "j1": ("sbuf", [128, 512], "float32"),
+    "jm": ("sbuf", [128, 512], "float32"),
     "dd": ("sbuf", [128, 512], "float32"),
     "de": ("sbuf", [128, 512], "float32"),
     "qq": ("sbuf", [128, 512], "float32"),
@@ -33,17 +33,14 @@ SCRATCH = {
     "cf": ("sbuf", [128, 64 * (NR - 1)], "float32"),
     "cs": ("sbuf", [128, 8], "float32"),
     "onef": ("sbuf", [128, 128], "float32"),
-    "b16": ("sbuf", [128, 8], "float32"),
     "psF": ("psum", [128, 512], "float32"),
     "psP": ("psum", [128, 512], "float32"),
     "psT": ("psum", [128, 512], "float32"),
     "psC": ("psum", [128, 512], "float32"),
     "fo": ("dram", [128, 64], "int32"),
-    "fin": ("dram", [NR - 1, 128, 64], "int32"),
 }
-SEMAPHORES = (["fo", "fl", "fa", "ci", "xl", "go", "aL", "aR", "sent", "yst", "ysl", "k_pid", "k_m16"]
-              + ["st%d" % k for k in range(NS)]
-              + ["v%d" % k for k in range(24)] + ["t_l", "t_c"]
+SEMAPHORES = (["fo", "fl", "fa", "xl", "go", "st0", "st1", "aL", "aR", "aQ", "sent", "yst", "ysl", "k_pid", "k_m16",
+               "s_jm", "t_l", "t_c"] + ["v%d" % k for k in range(24)]
               + ["vg%d" % k for k in range(NG)] + ["sg%d" % k for k in range(NG)])
 
 
@@ -53,6 +50,10 @@ def own_col(r):
 
 def land_col(src, dst):
     return own_col(dst) + SQ * (src - dst)
+
+
+def near(r):
+    return [d for d in (r - 1, r + 1) if 0 <= d < NR]
 
 
 def engines(mask):
@@ -71,21 +72,6 @@ def masks(core, dsts, topo):
     return out
 
 
-def send(g, core, topo, groups, local_sem):
-    tr = []
-    n = 0
-    for dsts, mask, src, dst, rsem in groups:
-        ids = []
-        for d in dsts:
-            rid, pid = topo.addr(d, core)
-            ids.append(DstId(rid=rid, pnc=pid))
-        tr.append(RemoteDMATransfer(dst_ids=ids, dma_engine_mask=mask, remote_sem=rsem, srcs=[src],
-                                    dsts=[dst] * len(ids), alu_op=0))
-        n += engines(mask)
-    g.remote_dma_fused(tr, local_sem=local_sem)
-    return n
-
-
 def rank_program(g, core, T, topo):
     r = T.rank_of(core)
     if r is None:
@@ -95,6 +81,19 @@ def rank_program(g, core, T, topo):
     V, A, E, Y = g.vector, g.scalar, g.tensor, g.sync
     own = own_col(r)
     ncols = own + SQ + (SQ if r < NR - 1 else 0)
+    sent = [0]
+
+    def send(groups):
+        tr = []
+        for ds, mask, src, dst, rsem in groups:
+            ids = []
+            for d in ds:
+                rid, pid = topo.addr(cores[d], core)
+                ids.append(DstId(rid=rid, pnc=pid))
+            tr.append(RemoteDMATransfer(dst_ids=ids, dma_engine_mask=mask, remote_sem=rsem, srcs=[src],
+                                        dsts=[dst] * len(ids), alu_op=0))
+            sent[0] += engines(mask)
+        g.remote_dma_fused(tr, local_sem=S.sent)
 
     def flag_groups(s):
         later = list(range(s + 1, NR))
@@ -104,50 +103,63 @@ def rank_program(g, core, T, topo):
             by.setdefault(mk[cores[d]], []).append(d)
         return sorted((m, ds) for m, ds in by.items())
 
-    def near(s):
-        return [d for d in (s + 1, s - 1) if 0 <= d < NR]
+    def chip_near(s):
+        return [d for d in near(s) if not topo.same_plane(cores[s], cores[d])]
+
+    def far_near(s):
+        return [d for d in near(s) if topo.same_plane(cores[s], cores[d])]
 
     def bulk_mask(s, d):
         return masks(cores[s], [cores[q] for q in near(s)], topo)[cores[d]]
 
-    for k in range(NS):
-        a, b = ST_CUTS[k], ST_CUTS[k + 1]
-        Y.dma_start(T.win[:, own + a:own + b], T.st[:, a:b]).then_inc(S["st%d" % k], 16)
-    Y.dma_start(T.win[:, X_CUTS[0]:X_CUTS[1]], T.x[:, X_CUTS[0]:X_CUTS[1]]).then_inc(S.xl, 16)
+    def st_piece(s, at, a, b):
+        lc = land_col(s, at)
+        return T.win[:, lc + a:lc + b]
+
+    def side(s, d):
+        return S.aL if s < d else S.aR
+
+    inner = len(far_near(r)) > 0
+    cuts = [0, RELAY, SQ] if inner else [0, SQ]
     if r < NR - 1:
         A.dma_start(T.fo[:], T.fl[:]).then_inc(S.fo, 16)
     A.dma_start(T.fls[:], T.fl[:]).then_inc(S.fl, 16)
+    for k in range(len(cuts) - 1):
+        a, b = cuts[k], cuts[k + 1]
+        Y.dma_start(T.win[:, own + a:own + b], T.st[:, a:b]).then_inc(S["st%d" % k], 16)
+    Y.dma_start(T.win[:, X_CUTS[0]:X_CUTS[1]], T.x[:, X_CUTS[0]:X_CUTS[1]]).then_inc(S.xl, 16)
 
     g.iota(T.pidx[:, 0:1], [[1, 1]], 0, 1).then_inc(S.k_pid, 1)
     g.iota(T.m16[:], [[0, 8], [1, 16]], 0, -1, allow_small_or_imprecise_dtypes=True).then_inc(S.k_m16, 1)
-    sent = 0
     if r < NR - 1:
         g.wait_ge(S.fo, 16)
-        sent += send(g, core, topo, [([cores[d] for d in ds], m, T.fo[:], T.fin[r], S.fa)
-                                     for m, ds in flag_groups(r)], S.sent)
-    for k in range(NS):
-        a, b = ST_CUTS[k], ST_CUTS[k + 1]
-        g.wait_ge(S["st%d" % k], 16)
-        gr = []
-        for d in near(r):
-            lc = land_col(r, d)
-            gr.append(([cores[d]], bulk_mask(r, d), T.win[:, own + a:own + b], T.win[:, lc + a:lc + b],
-                       S.aL if d > r else S.aR))
-        sent += send(g, core, topo, gr, S.sent)
-    g.sem_inc(S.go, 1)
+        send([(ds, m, T.fo[:], T.cin[:, 64 * r:64 * r + 64], S.fa) for m, ds in flag_groups(r)])
+    arrivals = []
+    on = chip_near(r)[0]
+    if inner:
+        far = far_near(r)[0]
+        g.wait_ge(S.st0, 16)
+        send([([on], bulk_mask(r, on), st_piece(r, r, 0, RELAY), st_piece(r, on, 0, RELAY), S.aQ)])
+        g.wait_ge(S.st1, 16)
+        send([([d], bulk_mask(r, d), st_piece(r, r, RELAY, SQ), st_piece(r, d, RELAY, SQ), side(r, d))
+              for d in (far, on)])
+        g.sem_inc(S.go, 1)
+        arrivals.append((S.aQ, engines(topo.mask(cores[chip_near(far)[0]], core))))
+        arrivals.append((side(far, r), engines(bulk_mask(far, r))))
+        arrivals.append((side(on, r), engines(topo.mask(cores[on], core))))
+    else:
+        g.wait_ge(S.st0, 16)
+        send([([on], topo.mask(core, cores[on]), st_piece(r, r, 0, SQ), st_piece(r, on, 0, SQ), side(r, on))])
+        g.sem_inc(S.go, 1)
+        far = far_near(on)[0]
+        g.wait_ge(S.aQ, engines(bulk_mask(on, r)))
+        send([([far], topo.mask(core, cores[far]), st_piece(on, r, 0, RELAY), st_piece(on, far, 0, RELAY), S.aQ)])
+        arrivals.append((S.aQ, engines(bulk_mask(on, r))))
+        arrivals.append((side(on, r), engines(bulk_mask(on, r))))
 
     Y.wait_ge(S.go, 1)
     for a, b in zip(X_CUTS[1:-1], X_CUTS[2:]):
         Y.dma_start(T.win[:, a:b], T.x[:, a:b]).then_inc(S.xl, 16)
-
-    fa = 0
-    for s in range(r):
-        for m, ds in flag_groups(s):
-            if r in ds:
-                fa += engines(m)
-    if r > 0:
-        A.wait_ge(S.fa, fa)
-        A.dma_start(T.cin[:, 0:64 * r], T.fin[0:r]).then_inc(S.ci, 16)
 
     cnt = [0]
 
@@ -157,8 +169,8 @@ def rank_program(g, core, T, topo):
         ins.then_inc(S[name], 1)
         return S[name]
 
-    s_one = inc(V.memset(T.one[:], 1.0))
     s_c16 = inc(V.memset(T.c16[:], 16.0))
+    s_one = inc(V.memset(T.one[:], 1.0))
     s_onef = inc(V.memset(T.onef[:], 1.0)) if r > 0 else None
     V.wait_ge(S.k_pid, 1)
     s = inc(V.tensor_scalar(T.pand[:, 0:1], T.pidx[:, 0:1], 15, None, Op.bitwise_and))
@@ -175,6 +187,9 @@ def rank_program(g, core, T, topo):
     V.wait_ge(s_fb, 1)
     s_rs = inc(V.tensor_tensor_scan(T.rs[:], T.fb[:], T.fb[:], 0.0, Op.add, Op.max))
 
+    A.wait_ge(s_j1, 1)
+    A.activation(T.jm[:], T.j1[:], Act.Copy, bias=float(-(W - SQ * max(r - 1, 0) + 16))).then_inc(S.s_jm, 1)
+
     for q in (s_sel, s_fb, s_one, s_rs, s_tri):
         E.wait_ge(q, 1)
     E.matmul(T.psF[:], T.sel[:], T.fb[:], True, True)
@@ -182,16 +197,22 @@ def rank_program(g, core, T, topo):
     E.matmul(T.psP[:], T.tri[:], T.fb[:], False, True).then_inc(S.t_l, 1)
 
     V.wait_ge(S.t_l, 1)
-    V.wait_ge(s_j1, 1)
-    s = inc(V.tensor_tensor(T.dd[:], T.psP[:], T.j1[:], Op.subtract))
+    V.wait_ge(S.s_jm, 1)
+    s = inc(V.tensor_tensor(T.dd[:], T.psP[:], T.jm[:], Op.subtract))
     V.wait_ge(s, 1)
     s = inc(V.tensor_tensor(T.de[:], T.dd[:], T.psF[:], Op.mult))
     V.wait_ge(s, 1)
-    s_q = inc(V.tensor_tensor(T.qq[:], T.de[:], T.j1[:], Op.add))
-
-    base = float(W - SQ * max(r - 1, 0) + 16)
+    V.wait_ge(s_j1, 1)
+    s = inc(V.tensor_tensor(T.qq[:], T.de[:], T.j1[:], Op.add))
+    last = T.qq
     if r > 0:
-        V.wait_ge(S.ci, 16)
+        fa = 0
+        for q in range(r):
+            for m, ds in flag_groups(q):
+                if r in ds:
+                    fa += engines(m)
+        s_q = s
+        V.wait_ge(S.fa, fa)
         s = inc(V.tensor_copy(T.cf[:, 0:64 * r], T.cin[:, 0:64 * r]))
         V.wait_ge(s, 1)
         s = inc(V.tensor_reduce(T.cs[:, 0:1], T.cf[:, 0:64 * r], AxisListType.X, Op.add))
@@ -199,32 +220,30 @@ def rank_program(g, core, T, topo):
         E.wait_ge(s_onef, 1)
         E.matmul(T.psC[:, 0:1], T.onef[:], T.cs[:, 0:1], True, True).then_inc(S.t_c, 1)
         V.wait_ge(S.t_c, 1)
-        s = inc(V.tensor_scalar(T.b16[:, 0:1], T.psC[:, 0:1], base, None, Op.add))
+        s = inc(V.tensor_scalar(T.psT[:], T.psF[:], T.psC[:, 0:1], None, Op.mult))
         V.wait_ge(s, 1)
-        base = T.b16[:, 0:1]
-    s = inc(V.tensor_scalar(T.psT[:], T.psF[:], base, None, Op.mult))
+        V.wait_ge(s_q, 1)
+        s = inc(V.tensor_tensor(T.t2[:], T.psT[:], T.qq[:], Op.add))
+        last = T.t2
     V.wait_ge(s, 1)
-    V.wait_ge(s_q, 1)
-    s = inc(V.tensor_tensor(T.t2[:], T.psT[:], T.qq[:], Op.add))
-    V.wait_ge(s, 1)
-    s_off = inc(V.tensor_scalar(T.off[:], T.t2[:], 16.0, None, Op.subtract))
+    s_off = inc(V.tensor_scalar(T.off[:], last[:], 16.0, None, Op.subtract))
 
     for q in (V, A):
         q.wait_ge(s_off, 1)
         q.wait_ge(S.xl, 16 * (len(X_CUTS) - 1))
-        for k in range(NS):
+        for k in range(len(cuts) - 1):
             q.wait_ge(S["st%d" % k], 16)
-        for d in near(r):
-            q.wait_ge(S.aR if d > r else S.aL, NS * engines(bulk_mask(d, r)))
+        for sem, n in arrivals:
+            q.wait_ge(sem, n)
     for k in range(NG):
-        a, b = G_CUTS[k], G_CUTS[k + 1]
+        a, b = V_CUTS[k], V_CUTS[k + 1]
         V.tensor_copy(T.yb[:, a:b], T.win[:, 0:ncols].indirect(T.off[:, a // 16:b // 16])).then_inc(S["vg%d" % k], 1)
         a, b = a + HALF, b + HALF
         A.activation(T.yb[:, a:b], T.win[:, 0:ncols].indirect(T.off[:, a // 16:b // 16]),
                      Act.Copy).then_inc(S["sg%d" % k], 1)
 
     for k in range(NG):
-        a, b = G_CUTS[k], G_CUTS[k + 1]
+        a, b = V_CUTS[k], V_CUTS[k + 1]
         Y.wait_ge(S["vg%d" % k], 1)
         Y.dma_start(T.y[:, a:b], T.yb[:, a:b]).then_inc(S.yst, 16)
         a, b = a + HALF, b + HALF
@@ -236,4 +255,4 @@ def rank_program(g, core, T, topo):
             A.dma_start(T.y[:, a:b], T.yb[:, a:b]).then_inc(S.ysl, 16)
     Y.wait_ge(S.yst, 16 * (2 * NG - 1))
     A.wait_ge(S.ysl, 16)
-    g.wait_ge(S.sent, sent)
+    g.wait_ge(S.sent, sent[0])

@@ -3,9 +3,9 @@ from concourse.mybir import dt, AluOpType as Op, AxisListType, ActivationFunctio
 
 NR, W, SQ = 4, 8192, 4096
 HALF = W // 2
-RELAY = 1024
-X_CUTS = [0, 6144, 8192]
-V_CUTS = [0, 1024, 2048, 3072, 4096]
+RELAY = 1152
+XE = 2304
+V_CUTS = [0, 1216, 2304, 3264, 4096]
 NG = len(V_CUTS) - 1
 
 SCRATCH = {
@@ -25,7 +25,6 @@ SCRATCH = {
     "j1": ("sbuf", [128, 512], "float32"),
     "jm": ("sbuf", [128, 512], "float32"),
     "dd": ("sbuf", [128, 512], "float32"),
-    "de": ("sbuf", [128, 512], "float32"),
     "qq": ("sbuf", [128, 512], "float32"),
     "t2": ("sbuf", [128, 512], "float32"),
     "off": ("sbuf", [128, 512], "uint16"),
@@ -35,17 +34,18 @@ SCRATCH = {
     "onef": ("sbuf", [128, 128], "float32"),
     "psF": ("psum", [128, 512], "float32"),
     "psP": ("psum", [128, 512], "float32"),
+    "psD": ("psum", [128, 512], "float32"),
     "psT": ("psum", [128, 512], "float32"),
     "psC": ("psum", [128, 512], "float32"),
     "fo": ("dram", [128, 64], "int32"),
 }
-SEMAPHORES = (["fo", "fl", "fa", "xl", "go", "st0", "st1", "aL", "aR", "aQ", "sent", "yst", "ysl", "k_pid", "k_m16",
-               "s_jm", "t_l", "t_c"] + ["v%d" % k for k in range(24)]
+SEMAPHORES = (["fo", "fl", "fa", "xe", "xf", "go", "st0", "st1", "aL", "aR", "aQ", "sent", "yst", "ysl", "k_pid",
+               "k_m16", "s_jm", "t_l", "t_c"] + ["v%d" % k for k in range(32)]
               + ["vg%d" % k for k in range(NG)] + ["sg%d" % k for k in range(NG)])
 
 
 def own_col(r):
-    return W + (SQ if r > 0 else 0)
+    return SQ if r > 0 else 0
 
 
 def land_col(src, dst):
@@ -80,7 +80,7 @@ def rank_program(g, core, T, topo):
     cores = list(T.cores)
     V, A, E, Y = g.vector, g.scalar, g.tensor, g.sync
     own = own_col(r)
-    ncols = own + SQ + (SQ if r < NR - 1 else 0)
+    nst = own + SQ + (SQ if r < NR - 1 else 0)
     sent = [0]
 
     def send(groups):
@@ -127,7 +127,7 @@ def rank_program(g, core, T, topo):
     for k in range(len(cuts) - 1):
         a, b = cuts[k], cuts[k + 1]
         Y.dma_start(T.win[:, own + a:own + b], T.st[:, a:b]).then_inc(S["st%d" % k], 16)
-    Y.dma_start(T.win[:, X_CUTS[0]:X_CUTS[1]], T.x[:, X_CUTS[0]:X_CUTS[1]]).then_inc(S.xl, 16)
+    Y.dma_start(T.win[:, nst:nst + 2 * XE], T.x[:, HALF - XE:HALF + XE]).then_inc(S.xe, 16)
 
     g.iota(T.pidx[:, 0:1], [[1, 1]], 0, 1).then_inc(S.k_pid, 1)
     g.iota(T.m16[:], [[0, 8], [1, 16]], 0, -1, allow_small_or_imprecise_dtypes=True).then_inc(S.k_m16, 1)
@@ -150,16 +150,18 @@ def rank_program(g, core, T, topo):
     else:
         g.wait_ge(S.st0, 16)
         send([([on], topo.mask(core, cores[on]), st_piece(r, r, 0, SQ), st_piece(r, on, 0, SQ), side(r, on))])
-        g.sem_inc(S.go, 1)
         far = far_near(on)[0]
         g.wait_ge(S.aQ, engines(bulk_mask(on, r)))
         send([([far], topo.mask(core, cores[far]), st_piece(on, r, 0, RELAY), st_piece(on, far, 0, RELAY), S.aQ)])
+        g.sem_inc(S.go, 1)
         arrivals.append((S.aQ, engines(bulk_mask(on, r))))
         arrivals.append((side(on, r), engines(bulk_mask(on, r))))
 
     Y.wait_ge(S.go, 1)
-    for a, b in zip(X_CUTS[1:-1], X_CUTS[2:]):
-        Y.dma_start(T.win[:, a:b], T.x[:, a:b]).then_inc(S.xl, 16)
+    n = HALF - XE
+    for h in (0, 1):
+        a, b = nst + 2 * XE + n * h, (HALF + XE) * h
+        Y.dma_start(T.win[:, a:a + n], T.x[:, b:b + n]).then_inc(S.xf, 16)
 
     cnt = [0]
 
@@ -169,7 +171,14 @@ def rank_program(g, core, T, topo):
         ins.then_inc(S[name], 1)
         return S[name]
 
-    s_c16 = inc(V.memset(T.c16[:], 16.0))
+    s_c16 = []
+    jumps = {HALF - XE: 16 - HALF - XE, HALF + XE: 16 + HALF - XE}
+    at = 0
+    for j in sorted(jumps) + [W]:
+        s_c16.append(inc(V.memset(T.c16[:, at:j // 16], 16.0)))
+        if j < W:
+            s_c16.append(inc(V.memset(T.c16[:, j // 16:j // 16 + 1], float(jumps[j]))))
+        at = j // 16 + 1
     s_one = inc(V.memset(T.one[:], 1.0))
     s_onef = inc(V.memset(T.onef[:], 1.0)) if r > 0 else None
     V.wait_ge(S.k_pid, 1)
@@ -178,9 +187,10 @@ def rank_program(g, core, T, topo):
     s_sel = inc(V.tensor_scalar(T.sel[:], T.m16[:], 0.0, None, Op.is_equal))
     s_tri = inc(V.tensor_scalar(T.tri[:], T.m16[:], 0.0, -1.0, Op.is_le, Op.mult))
     V.wait_ge(s, 1)
-    s = inc(V.tensor_copy(T.acol[:, 0:1], T.pand[:, 0:1]))
+    s = inc(V.tensor_scalar(T.acol[:, 0:1], T.pand[:, 0:1], float(nst + 2 * XE), None, Op.add))
     V.wait_ge(s, 1)
-    V.wait_ge(s_c16, 1)
+    for q in s_c16:
+        V.wait_ge(q, 1)
     s_j1 = inc(V.tensor_tensor_scan(T.j1[:], T.c16[:], T.c16[:], T.acol[:, 0:1], Op.add, Op.max))
     V.wait_ge(S.fl, 16)
     s_fb = inc(V.tensor_copy(T.fb[:], T.fls[:]))
@@ -188,7 +198,7 @@ def rank_program(g, core, T, topo):
     s_rs = inc(V.tensor_tensor_scan(T.rs[:], T.fb[:], T.fb[:], 0.0, Op.add, Op.max))
 
     A.wait_ge(s_j1, 1)
-    A.activation(T.jm[:], T.j1[:], Act.Copy, bias=float(-(W - SQ * max(r - 1, 0) + 16))).then_inc(S.s_jm, 1)
+    A.activation(T.jm[:], T.j1[:], Act.Copy, bias=float(-(16 - SQ * max(r - 1, 0)))).then_inc(S.s_jm, 1)
 
     for q in (s_sel, s_fb, s_one, s_rs, s_tri):
         E.wait_ge(q, 1)
@@ -200,10 +210,10 @@ def rank_program(g, core, T, topo):
     V.wait_ge(S.s_jm, 1)
     s = inc(V.tensor_tensor(T.dd[:], T.psP[:], T.jm[:], Op.subtract))
     V.wait_ge(s, 1)
-    s = inc(V.tensor_tensor(T.de[:], T.dd[:], T.psF[:], Op.mult))
+    s = inc(V.tensor_tensor(T.psD[:], T.dd[:], T.psF[:], Op.mult))
     V.wait_ge(s, 1)
     V.wait_ge(s_j1, 1)
-    s = inc(V.tensor_tensor(T.qq[:], T.de[:], T.j1[:], Op.add))
+    s = inc(V.tensor_tensor(T.qq[:], T.psD[:], T.j1[:], Op.add))
     last = T.qq
     if r > 0:
         fa = 0
@@ -230,29 +240,39 @@ def rank_program(g, core, T, topo):
 
     for q in (V, A):
         q.wait_ge(s_off, 1)
-        q.wait_ge(S.xl, 16 * (len(X_CUTS) - 1))
+        q.wait_ge(S.xe, 16)
         for k in range(len(cuts) - 1):
             q.wait_ge(S["st%d" % k], 16)
         for sem, n in arrivals:
             q.wait_ge(sem, n)
     for k in range(NG):
         a, b = V_CUTS[k], V_CUTS[k + 1]
-        V.tensor_copy(T.yb[:, a:b], T.win[:, 0:ncols].indirect(T.off[:, a // 16:b // 16])).then_inc(S["vg%d" % k], 1)
-        a, b = a + HALF, b + HALF
+        ncols = nst + (2 * XE if b <= XE else W)
+        if a == XE:
+            V.wait_ge(S.xf, 32)
+            A.wait_ge(S.xf, 32)
+        va, vb = HALF - b, HALF - a
+        V.tensor_copy(T.yb[:, va:vb],
+                      T.win[:, 0:ncols].indirect(T.off[:, va // 16:vb // 16])).then_inc(S["vg%d" % k], 1)
+        a, b = HALF + a, HALF + b
         A.activation(T.yb[:, a:b], T.win[:, 0:ncols].indirect(T.off[:, a // 16:b // 16]),
                      Act.Copy).then_inc(S["sg%d" % k], 1)
 
-    for k in range(NG):
+    a = V_CUTS[1]
+    Y.wait_ge(S.vg0, 1)
+    Y.wait_ge(S.sg0, 1)
+    Y.dma_start(T.y[:, HALF - a:HALF + a], T.yb[:, HALF - a:HALF + a]).then_inc(S.yst, 16)
+    for k in range(1, NG):
         a, b = V_CUTS[k], V_CUTS[k + 1]
         Y.wait_ge(S["vg%d" % k], 1)
-        Y.dma_start(T.y[:, a:b], T.yb[:, a:b]).then_inc(S.yst, 16)
-        a, b = a + HALF, b + HALF
+        Y.dma_start(T.y[:, HALF - b:HALF - a], T.yb[:, HALF - b:HALF - a]).then_inc(S.yst, 16)
+        a, b = HALF + a, HALF + b
         if k < NG - 1:
             Y.wait_ge(S["sg%d" % k], 1)
             Y.dma_start(T.y[:, a:b], T.yb[:, a:b]).then_inc(S.yst, 16)
         else:
             A.wait_ge(S["sg%d" % k], 1)
             A.dma_start(T.y[:, a:b], T.yb[:, a:b]).then_inc(S.ysl, 16)
-    Y.wait_ge(S.yst, 16 * (2 * NG - 1))
+    Y.wait_ge(S.yst, 16 * (2 * NG - 2))
     A.wait_ge(S.ysl, 16)
     g.wait_ge(S.sent, sent[0])

@@ -2,11 +2,14 @@ from concourse.bass import DstId, RemoteDMATransfer
 from concourse.mybir import dt, AluOpType as Op, AxisListType, ActivationFunctionType as Act
 
 NR, W, SQ = 4, 8192, 4096
-HALF = W // 2
-RELAY = 1152
-XE = 2304
-V_CUTS = [0, 1216, 2304, 3264, 4096]
-NG = len(V_CUTS) - 1
+U = [0, 1408, 2688, 4736, 6784, W]
+NG = len(U) - 1
+X = [0, U[1], U[2], U[3], W]
+NX = len(X) - 1
+NEAR = 2
+EARLY = 2
+D = [0, U[1], U[2], SQ]
+assert D[1] - D[0] == D[3] - D[2]
 
 SCRATCH = {
     "win": ("sbuf", [128, W + 3 * SQ], "bfloat16"),
@@ -27,29 +30,44 @@ SCRATCH = {
     "dd": ("sbuf", [128, 512], "float32"),
     "qq": ("sbuf", [128, 512], "float32"),
     "t2": ("sbuf", [128, 512], "float32"),
-    "off": ("sbuf", [128, 512], "uint16"),
     "cin": ("sbuf", [128, 64 * (NR - 1)], "int32"),
     "cf": ("sbuf", [128, 64 * (NR - 1)], "float32"),
     "cs": ("sbuf", [128, 8], "float32"),
     "onef": ("sbuf", [128, 128], "float32"),
-    "psF": ("psum", [128, 512], "float32"),
-    "psP": ("psum", [128, 512], "float32"),
+    "psF0": ("psum", [128, 512], "float32"),
+    "psF1": ("psum", [128, 512], "float32"),
+    "psP0": ("psum", [128, 512], "float32"),
+    "psP1": ("psum", [128, 512], "float32"),
     "psD": ("psum", [128, 512], "float32"),
     "psT": ("psum", [128, 512], "float32"),
     "psC": ("psum", [128, 512], "float32"),
     "fo": ("dram", [128, 64], "int32"),
 }
-SEMAPHORES = (["fo", "fl", "fa", "xe", "xf", "go", "st0", "st1", "aL", "aR", "aQ", "sent", "yst", "ysl", "k_pid",
-               "k_m16", "s_jm", "t_l", "t_c"] + ["v%d" % k for k in range(32)]
+for _k in range(NG):
+    SCRATCH["off%d" % _k] = ("sbuf", [128, 512], "uint16")
+SEMAPHORES = (["fo", "fl", "fa", "go", "st", "aQ", "o1", "f1", "f2", "sent", "yst", "k_pid", "k_m16", "s_jm",
+               "t_l0", "t_l1", "t_c"] + ["v%d" % k for k in range(48)] + ["x%d" % k for k in range(NX)]
               + ["vg%d" % k for k in range(NG)] + ["sg%d" % k for k in range(NG)])
 
 
-def own_col(r):
-    return SQ if r > 0 else 0
+def first_part(r):
+    return max(r - 1, 0)
 
 
-def land_col(src, dst):
-    return own_col(dst) + SQ * (src - dst)
+def parts(r):
+    return min(r + 1, NR - 1) - first_part(r) + 1
+
+
+def least(r):
+    return SQ * max(min(r, NR - 1) - 1, 0)
+
+
+def most(r):
+    return min(SQ * (r + 1), SQ * NR, W * r)
+
+
+def stream_range(r, ja, jb):
+    return max(least(r), least(r + 1) - (W - ja)), min(most(r) + jb, most(r + 1))
 
 
 def near(r):
@@ -79,8 +97,6 @@ def rank_program(g, core, T, topo):
     S = T.sem
     cores = list(T.cores)
     V, A, E, Y = g.vector, g.scalar, g.tensor, g.sync
-    own = own_col(r)
-    nst = own + SQ + (SQ if r < NR - 1 else 0)
     sent = [0]
 
     def send(groups):
@@ -112,56 +128,122 @@ def rank_program(g, core, T, topo):
     def bulk_mask(s, d):
         return masks(cores[s], [cores[q] for q in near(s)], topo)[cores[d]]
 
+    def all_mask(s, d):
+        return topo.mask(cores[s], cores[d])
+
+    inner = r if far_near(r) else chip_near(r)[0]
+    far = far_near(inner)[0]
+    on = chip_near(r)[0]
+
+    def up(s):
+        q = s if far_near(s) else chip_near(s)[0]
+        return far_near(q)[0] > q
+
+    def layout(s):
+        n = W + parts(s) * SQ
+        return n, X[NEAR] if up(s) else n - X[NEAR] - parts(s) * SQ
+
+    def ucols(s, a, b):
+        return (a, b) if up(s) else (W - b, W - a)
+
+    def x_place(k):
+        n, _ = layout(r)
+        p = X[NEAR] - X[k + 1] if k < NEAR else parts(r) * SQ + X[k]
+        return p if up(r) else n - p - (X[k + 1] - X[k])
+
+    def st_place(s, at):
+        return layout(at)[1] + SQ * (s - first_part(at))
+
     def st_piece(s, at, a, b):
-        lc = land_col(s, at)
+        lc = st_place(s, at)
         return T.win[:, lc + a:lc + b]
 
-    def side(s, d):
-        return S.aL if s < d else S.aR
+    def cut(s, a, b):
+        return (SQ - b, SQ - a) if up(s) else (a, b)
 
-    inner = len(far_near(r)) > 0
-    cuts = [0, RELAY, SQ] if inner else [0, SQ]
+    def hasty(s):
+        d = chip_near(s)[0]
+        a, b = stream_range(d, *ucols(d, U[0], U[1]))
+        return a <= SQ * s and SQ * (s + 1) <= b
+
     if r < NR - 1:
         A.dma_start(T.fo[:], T.fl[:]).then_inc(S.fo, 16)
-    A.dma_start(T.fls[:], T.fl[:]).then_inc(S.fl, 16)
-    for k in range(len(cuts) - 1):
-        a, b = cuts[k], cuts[k + 1]
-        Y.dma_start(T.win[:, own + a:own + b], T.st[:, a:b]).then_inc(S["st%d" % k], 16)
-    Y.dma_start(T.win[:, nst:nst + 2 * XE], T.x[:, HALF - XE:HALF + XE]).then_inc(S.xe, 16)
+    Y.dma_start(T.fls[:], T.fl[:]).then_inc(S.fl, 16)
+    regions = []
+    own = st_place(r, r)
+    Y.dma_start(T.win[:, own:own + SQ], T.st[:]).then_inc(S.st, 16)
+    regions.append((own, own + SQ, S.st, 16))
+
+    def load_x(k):
+        p, (a, b) = x_place(k), ucols(r, X[k], X[k + 1])
+        Y.dma_start(T.win[:, p:p + b - a], T.x[:, a:b]).then_inc(S["x%d" % k], 16)
+        regions.append((p, p + b - a, S["x%d" % k], 16))
+
+    for k in range(EARLY):
+        load_x(k)
 
     g.iota(T.pidx[:, 0:1], [[1, 1]], 0, 1).then_inc(S.k_pid, 1)
     g.iota(T.m16[:], [[0, 8], [1, 16]], 0, -1, allow_small_or_imprecise_dtypes=True).then_inc(S.k_m16, 1)
     if r < NR - 1:
         g.wait_ge(S.fo, 16)
         send([(ds, m, T.fo[:], T.cin[:, 64 * r:64 * r + 64], S.fa) for m, ds in flag_groups(r)])
-    arrivals = []
-    on = chip_near(r)[0]
-    if inner:
-        far = far_near(r)[0]
-        g.wait_ge(S.st0, 16)
-        send([([on], bulk_mask(r, on), st_piece(r, r, 0, RELAY), st_piece(r, on, 0, RELAY), S.aQ)])
-        g.wait_ge(S.st1, 16)
-        send([([d], bulk_mask(r, d), st_piece(r, r, RELAY, SQ), st_piece(r, d, RELAY, SQ), side(r, d))
-              for d in (far, on)])
-        g.sem_inc(S.go, 1)
-        arrivals.append((S.aQ, engines(topo.mask(cores[chip_near(far)[0]], core))))
-        arrivals.append((side(far, r), engines(bulk_mask(far, r))))
-        arrivals.append((side(on, r), engines(topo.mask(cores[on], core))))
-    else:
-        g.wait_ge(S.st0, 16)
-        send([([on], topo.mask(core, cores[on]), st_piece(r, r, 0, SQ), st_piece(r, on, 0, SQ), side(r, on))])
-        far = far_near(on)[0]
-        g.wait_ge(S.aQ, engines(bulk_mask(on, r)))
-        send([([far], topo.mask(core, cores[far]), st_piece(on, r, 0, RELAY), st_piece(on, far, 0, RELAY), S.aQ)])
-        g.sem_inc(S.go, 1)
-        arrivals.append((S.aQ, engines(bulk_mask(on, r))))
-        arrivals.append((side(on, r), engines(bulk_mask(on, r))))
 
+    def piece(s, d, a, b, mask, sem):
+        return [d], mask, st_piece(s, r, a, b), st_piece(s, d, a, b), sem
+
+    def arrives(s, a, b, sem, n):
+        p = st_place(s, r)
+        regions.append((p + a, p + b, sem, n))
+
+    first, middle, last, rest = (0, D[1]), (D[1], D[2]), (D[2], D[3]), (0, D[2])
+    g.wait_ge(S.st, 16)
+    if r == inner:
+        mf, mo = bulk_mask(r, far), bulk_mask(r, on)
+        send([piece(r, far, *cut(r, *first), mf, S.f1), piece(r, on, *cut(r, *last), mo, S.aQ)])
+        if hasty(r):
+            send([piece(r, on, *cut(r, *rest), all_mask(r, on), S.o1)])
+            send([piece(r, far, *cut(r, *middle), mf, S.f2)])
+        else:
+            send([piece(r, far, *cut(r, *middle), mf, S.f2), piece(r, on, *cut(r, *middle), mo, S.o1)])
+            send([piece(r, on, *cut(r, *first), all_mask(r, on), S.o1)])
+        arrives(far, *cut(far, *first), S.f1, engines(bulk_mask(far, r)))
+        arrives(far, *cut(far, *middle), S.f2, engines(bulk_mask(far, r)))
+        arrives(far, *cut(far, *last), S.aQ, engines(all_mask(chip_near(far)[0], r)))
+        arrives(on, 0, SQ, S.o1, engines(all_mask(on, r)))
+    else:
+        send([piece(r, on, 0, SQ, all_mask(r, on), S.o1)])
+        n = engines(bulk_mask(on, r))
+        g.wait_ge(S.aQ, n)
+        send([piece(on, far, *cut(on, *last), all_mask(r, far), S.aQ)])
+        arrives(on, *cut(on, *last), S.aQ, n)
+        arrives(on, *cut(on, *rest), S.o1, engines(all_mask(on, r)) + (0 if hasty(on) else n))
+    g.sem_inc(S.go, 1)
     Y.wait_ge(S.go, 1)
-    n = HALF - XE
-    for h in (0, 1):
-        a, b = nst + 2 * XE + n * h, (HALF + XE) * h
-        Y.dma_start(T.win[:, a:a + n], T.x[:, b:b + n]).then_inc(S.xf, 16)
+    for k in range(EARLY, NX):
+        load_x(k)
+
+    blocks = sorted((ucols(r, X[k], X[k + 1]), x_place(k)) for k in range(NX))
+
+    def place(j):
+        for (a, b), p in blocks:
+            if a <= j < b:
+                return p + j - a
+
+    zero = layout(r)[1] - SQ * first_part(r)
+    wins = []
+    lo = hi = None
+    for k in range(NG):
+        ja, jb = ucols(r, U[k], U[k + 1])
+        sa, sb = stream_range(r, ja, jb)
+        ends = [(zero + sa, zero + sb)]
+        for (a, b), p in blocks:
+            if max(a, ja) < min(b, jb):
+                ends.append((p + max(a, ja) - a, p + min(b, jb) - a))
+        lo = min([e[0] for e in ends] + ([lo] if k else []))
+        hi = max([e[1] for e in ends] + ([hi] if k else []))
+        touched = [(p, e) for p, e, sem, n in regions if max(p, lo) < min(e, hi)]
+        lo, hi = min(p for p, e in touched), max(e for p, e in touched)
+        wins.append((lo, hi))
 
     cnt = [0]
 
@@ -172,12 +254,11 @@ def rank_program(g, core, T, topo):
         return S[name]
 
     s_c16 = []
-    jumps = {HALF - XE: 16 - HALF - XE, HALF + XE: 16 + HALF - XE}
     at = 0
-    for j in sorted(jumps) + [W]:
+    for j in [a for (a, b), p in blocks if a > 0 and place(a) != place(a - 16) + 16] + [W]:
         s_c16.append(inc(V.memset(T.c16[:, at:j // 16], 16.0)))
         if j < W:
-            s_c16.append(inc(V.memset(T.c16[:, j // 16:j // 16 + 1], float(jumps[j]))))
+            s_c16.append(inc(V.memset(T.c16[:, j // 16:j // 16 + 1], float(place(j) - place(j - 16)))))
         at = j // 16 + 1
     s_one = inc(V.memset(T.one[:], 1.0))
     s_onef = inc(V.memset(T.onef[:], 1.0)) if r > 0 else None
@@ -187,7 +268,7 @@ def rank_program(g, core, T, topo):
     s_sel = inc(V.tensor_scalar(T.sel[:], T.m16[:], 0.0, None, Op.is_equal))
     s_tri = inc(V.tensor_scalar(T.tri[:], T.m16[:], 0.0, -1.0, Op.is_le, Op.mult))
     V.wait_ge(s, 1)
-    s = inc(V.tensor_scalar(T.acol[:, 0:1], T.pand[:, 0:1], float(nst + 2 * XE), None, Op.add))
+    s = inc(V.tensor_scalar(T.acol[:, 0:1], T.pand[:, 0:1], float(place(0)), None, Op.add))
     V.wait_ge(s, 1)
     for q in s_c16:
         V.wait_ge(q, 1)
@@ -198,30 +279,69 @@ def rank_program(g, core, T, topo):
     s_rs = inc(V.tensor_tensor_scan(T.rs[:], T.fb[:], T.fb[:], 0.0, Op.add, Op.max))
 
     A.wait_ge(s_j1, 1)
-    A.activation(T.jm[:], T.j1[:], Act.Copy, bias=float(-(16 - SQ * max(r - 1, 0)))).then_inc(S.s_jm, 1)
+    A.activation(T.jm[:], T.j1[:], Act.Copy, bias=float(-(16 + zero))).then_inc(S.s_jm, 1)
+
+    chunks = [[0], list(range(1, NG))]
+
+    def span(ks):
+        cols = [ucols(r, U[k], U[k + 1]) for k in ks]
+        return min(a for a, b in cols) // 16, max(b for a, b in cols) // 16
 
     for q in (s_sel, s_fb, s_one, s_rs, s_tri):
         E.wait_ge(q, 1)
-    E.matmul(T.psF[:], T.sel[:], T.fb[:], True, True)
-    E.matmul(T.psP[:], T.one[:], T.rs[:], True, False)
-    E.matmul(T.psP[:], T.tri[:], T.fb[:], False, True).then_inc(S.t_l, 1)
+    for h in (0, 1):
+        a, b = span(chunks[h])
+        F, P = T["psF%d" % h], T["psP%d" % h]
+        E.matmul(F[:, a:b], T.sel[:], T.fb[:, a:b], True, True)
+        E.matmul(P[:, a:b], T.one[:], T.rs[:, a:b], True, False)
+        E.matmul(P[:, a:b], T.tri[:], T.fb[:, a:b], False, True).then_inc(S["t_l%d" % h], 1)
 
-    V.wait_ge(S.t_l, 1)
-    V.wait_ge(S.s_jm, 1)
-    s = inc(V.tensor_tensor(T.dd[:], T.psP[:], T.jm[:], Op.subtract))
-    V.wait_ge(s, 1)
-    s = inc(V.tensor_tensor(T.psD[:], T.dd[:], T.psF[:], Op.mult))
-    V.wait_ge(s, 1)
-    V.wait_ge(s_j1, 1)
-    s = inc(V.tensor_tensor(T.qq[:], T.psD[:], T.j1[:], Op.add))
-    last = T.qq
-    if r > 0:
+    def before_c(h):
+        a, b = span(chunks[h])
+        V.wait_ge(S["t_l%d" % h], 1)
+        if h == 0:
+            V.wait_ge(S.s_jm, 1)
+            V.wait_ge(s_j1, 1)
+        s = inc(V.tensor_tensor(T.dd[:, a:b], T["psP%d" % h][:, a:b], T.jm[:, a:b], Op.subtract))
+        V.wait_ge(s, 1)
+        s = inc(V.tensor_tensor(T.psD[:, a:b], T.dd[:, a:b], T["psF%d" % h][:, a:b], Op.mult))
+        V.wait_ge(s, 1)
+        s = inc(V.tensor_tensor(T.qq[:, a:b], T.psD[:, a:b], T.j1[:, a:b], Op.add))
+        V.wait_ge(s, 1)
+
+    offs = {}
+
+    def after_c(h):
+        src = T.qq
+        if r > 0:
+            a, b = span(chunks[h])
+            s = inc(V.tensor_scalar(T.psT[:, a:b], T["psF%d" % h][:, a:b], T.psC[:, 0:1], None, Op.mult))
+            V.wait_ge(s, 1)
+            s = inc(V.tensor_tensor(T.t2[:, a:b], T.psT[:, a:b], T.qq[:, a:b], Op.add))
+            V.wait_ge(s, 1)
+            src = T.t2
+        ks = chunks[h]
+        while ks:
+            same = [k for k in ks if wins[k][0] == wins[ks[0]][0]]
+            a, b = span(same)
+            t = T["off%d" % same[0]]
+            q = inc(V.tensor_scalar(t[:, 0:b - a], src[:, a:b], float(16 + wins[same[0]][0]), None, Op.subtract))
+            for k in same:
+                offs[k] = (q, t, a)
+            ks = ks[len(same):]
+
+    before_c(0)
+    if r == 0:
+        after_c(0)
+        before_c(1)
+        after_c(1)
+    else:
+        before_c(1)
         fa = 0
         for q in range(r):
             for m, ds in flag_groups(q):
                 if r in ds:
                     fa += engines(m)
-        s_q = s
         V.wait_ge(S.fa, fa)
         s = inc(V.tensor_copy(T.cf[:, 0:64 * r], T.cin[:, 0:64 * r]))
         V.wait_ge(s, 1)
@@ -230,49 +350,30 @@ def rank_program(g, core, T, topo):
         E.wait_ge(s_onef, 1)
         E.matmul(T.psC[:, 0:1], T.onef[:], T.cs[:, 0:1], True, True).then_inc(S.t_c, 1)
         V.wait_ge(S.t_c, 1)
-        s = inc(V.tensor_scalar(T.psT[:], T.psF[:], T.psC[:, 0:1], None, Op.mult))
-        V.wait_ge(s, 1)
-        V.wait_ge(s_q, 1)
-        s = inc(V.tensor_tensor(T.t2[:], T.psT[:], T.qq[:], Op.add))
-        last = T.t2
-    V.wait_ge(s, 1)
-    s_off = inc(V.tensor_scalar(T.off[:], last[:], 16.0, None, Op.subtract))
+        after_c(0)
+        after_c(1)
 
-    for q in (V, A):
-        q.wait_ge(s_off, 1)
-        q.wait_ge(S.xe, 16)
-        for k in range(len(cuts) - 1):
-            q.wait_ge(S["st%d" % k], 16)
-        for sem, n in arrivals:
-            q.wait_ge(sem, n)
+    there = []
     for k in range(NG):
-        a, b = V_CUTS[k], V_CUTS[k + 1]
-        ncols = nst + (2 * XE if b <= XE else W)
-        if a == XE:
-            V.wait_ge(S.xf, 32)
-            A.wait_ge(S.xf, 32)
-        va, vb = HALF - b, HALF - a
-        V.tensor_copy(T.yb[:, va:vb],
-                      T.win[:, 0:ncols].indirect(T.off[:, va // 16:vb // 16])).then_inc(S["vg%d" % k], 1)
-        a, b = HALF + a, HALF + b
-        A.activation(T.yb[:, a:b], T.win[:, 0:ncols].indirect(T.off[:, a // 16:b // 16]),
-                     Act.Copy).then_inc(S["sg%d" % k], 1)
+        lo, hi = wins[k]
+        new = [(p, sem, n) for p, e, sem, n in regions if max(p, lo) < min(e, hi) and p not in there]
+        there += [p for p, sem, n in new]
+        s_off, t, c0 = offs[k]
+        ja, jb = ucols(r, U[k], U[k + 1])
+        jm = ja + (jb - ja) // 64 * 32
+        for q in (V, A):
+            q.wait_ge(s_off, 1)
+            for p, sem, n in new:
+                q.wait_ge(sem, n)
+        V.tensor_copy(T.yb[:, ja:jm], T.win[:, lo:hi].indirect(t[:, ja // 16 - c0:jm // 16 - c0])
+                      ).then_inc(S["vg%d" % k], 1)
+        A.activation(T.yb[:, jm:jb], T.win[:, lo:hi].indirect(t[:, jm // 16 - c0:jb // 16 - c0]), Act.Copy
+                     ).then_inc(S["sg%d" % k], 1)
 
-    a = V_CUTS[1]
-    Y.wait_ge(S.vg0, 1)
-    Y.wait_ge(S.sg0, 1)
-    Y.dma_start(T.y[:, HALF - a:HALF + a], T.yb[:, HALF - a:HALF + a]).then_inc(S.yst, 16)
-    for k in range(1, NG):
-        a, b = V_CUTS[k], V_CUTS[k + 1]
+    for k in range(NG):
+        ja, jb = ucols(r, U[k], U[k + 1])
         Y.wait_ge(S["vg%d" % k], 1)
-        Y.dma_start(T.y[:, HALF - b:HALF - a], T.yb[:, HALF - b:HALF - a]).then_inc(S.yst, 16)
-        a, b = HALF + a, HALF + b
-        if k < NG - 1:
-            Y.wait_ge(S["sg%d" % k], 1)
-            Y.dma_start(T.y[:, a:b], T.yb[:, a:b]).then_inc(S.yst, 16)
-        else:
-            A.wait_ge(S["sg%d" % k], 1)
-            A.dma_start(T.y[:, a:b], T.yb[:, a:b]).then_inc(S.ysl, 16)
-    Y.wait_ge(S.yst, 16 * (2 * NG - 2))
-    A.wait_ge(S.ysl, 16)
+        Y.wait_ge(S["sg%d" % k], 1)
+        Y.dma_start(T.y[:, ja:jb], T.yb[:, ja:jb]).then_inc(S.yst, 16)
+    Y.wait_ge(S.yst, 16 * NG)
     g.wait_ge(S.sent, sent[0])

from concourse.bass import DstId, RemoteDMATransfer
from concourse.mybir import dt, AluOpType as Op, AxisListType, ActivationFunctionType as Act

NR, W, SQ = 4, 8192, 4096
U = [0, 1408, 2688, 4736, 6784, W]
NG = len(U) - 1
X = [0, U[1], U[2], U[3], W]
NX = len(X) - 1
NEAR = 2
EARLY = 2
D = [0, U[1], U[2], SQ]
assert D[1] - D[0] == D[3] - D[2]

SCRATCH = {
    "win": ("sbuf", [128, W + 3 * SQ], "bfloat16"),
    "yb": ("sbuf", [128, W], "bfloat16"),
    "fls": ("sbuf", [16, 512], "int32"),
    "fb": ("sbuf", [16, 512], "bfloat16"),
    "rs": ("sbuf", [16, 512], "float16"),
    "m16": ("sbuf", [16, 128], "float32"),
    "sel": ("sbuf", [16, 128], "bfloat16"),
    "tri": ("sbuf", [16, 128], "bfloat16"),
    "one": ("sbuf", [16, 128], "bfloat16"),
    "pidx": ("sbuf", [128, 8], "int32"),
    "pand": ("sbuf", [128, 8], "int32"),
    "acol": ("sbuf", [128, 8], "float32"),
    "c16": ("sbuf", [128, 512], "float32"),
    "j1": ("sbuf", [128, 512], "float32"),
    "jm": ("sbuf", [128, 512], "float32"),
    "dd": ("sbuf", [128, 512], "float32"),
    "qq": ("sbuf", [128, 512], "float32"),
    "t2": ("sbuf", [128, 512], "float32"),
    "cin": ("sbuf", [128, 64 * (NR - 1)], "int32"),
    "cf": ("sbuf", [128, 64 * (NR - 1)], "float32"),
    "cs": ("sbuf", [128, 8], "float32"),
    "onef": ("sbuf", [128, 128], "float32"),
    "psF0": ("psum", [128, 512], "float32"),
    "psF1": ("psum", [128, 512], "float32"),
    "psP0": ("psum", [128, 512], "float32"),
    "psP1": ("psum", [128, 512], "float32"),
    "psD": ("psum", [128, 512], "float32"),
    "psT": ("psum", [128, 512], "float32"),
    "psC": ("psum", [128, 512], "float32"),
    "fo": ("dram", [128, 64], "int32"),
}
for _k in range(NG):
    SCRATCH["off%d" % _k] = ("sbuf", [128, 512], "uint16")
SEMAPHORES = (["fo", "fl", "fa", "go", "st", "aQ", "o1", "f1", "f2", "sent", "yst", "k_pid", "k_m16", "s_jm",
               "t_l0", "t_l1", "t_c"] + ["v%d" % k for k in range(48)] + ["x%d" % k for k in range(NX)]
              + ["vg%d" % k for k in range(NG)] + ["sg%d" % k for k in range(NG)])


def first_part(r):
    return max(r - 1, 0)


def parts(r):
    return min(r + 1, NR - 1) - first_part(r) + 1


def least(r):
    return SQ * max(min(r, NR - 1) - 1, 0)


def most(r):
    return min(SQ * (r + 1), SQ * NR, W * r)


def stream_range(r, ja, jb):
    return max(least(r), least(r + 1) - (W - ja)), min(most(r) + jb, most(r + 1))


def near(r):
    return [d for d in (r - 1, r + 1) if 0 <= d < NR]


def engines(mask):
    return bin(mask).count("1")


def masks(core, dsts, topo):
    off = 0
    for d in dsts:
        if topo.same_plane(core, d):
            off |= topo.mask(core, d)
    out = {}
    for d in dsts:
        m = topo.mask(core, d)
        out[d] = m if topo.same_plane(core, d) else m & ~off
    return out


def rank_program(g, core, T, topo):
    r = T.rank_of(core)
    if r is None:
        return
    S = T.sem
    cores = list(T.cores)
    V, A, E, Y = g.vector, g.scalar, g.tensor, g.sync
    sent = [0]

    def send(groups):
        tr = []
        for ds, mask, src, dst, rsem in groups:
            ids = []
            for d in ds:
                rid, pid = topo.addr(cores[d], core)
                ids.append(DstId(rid=rid, pnc=pid))
            tr.append(RemoteDMATransfer(dst_ids=ids, dma_engine_mask=mask, remote_sem=rsem, srcs=[src],
                                        dsts=[dst] * len(ids), alu_op=0))
            sent[0] += engines(mask)
        g.remote_dma_fused(tr, local_sem=S.sent)

    def flag_groups(s):
        later = list(range(s + 1, NR))
        mk = masks(cores[s], [cores[d] for d in later], topo)
        by = {}
        for d in later:
            by.setdefault(mk[cores[d]], []).append(d)
        return sorted((m, ds) for m, ds in by.items())

    def chip_near(s):
        return [d for d in near(s) if not topo.same_plane(cores[s], cores[d])]

    def far_near(s):
        return [d for d in near(s) if topo.same_plane(cores[s], cores[d])]

    def bulk_mask(s, d):
        return masks(cores[s], [cores[q] for q in near(s)], topo)[cores[d]]

    def all_mask(s, d):
        return topo.mask(cores[s], cores[d])

    inner = r if far_near(r) else chip_near(r)[0]
    far = far_near(inner)[0]
    on = chip_near(r)[0]

    def up(s):
        q = s if far_near(s) else chip_near(s)[0]
        return far_near(q)[0] > q

    def layout(s):
        n = W + parts(s) * SQ
        return n, X[NEAR] if up(s) else n - X[NEAR] - parts(s) * SQ

    def ucols(s, a, b):
        return (a, b) if up(s) else (W - b, W - a)

    def x_place(k):
        n, _ = layout(r)
        p = X[NEAR] - X[k + 1] if k < NEAR else parts(r) * SQ + X[k]
        return p if up(r) else n - p - (X[k + 1] - X[k])

    def st_place(s, at):
        return layout(at)[1] + SQ * (s - first_part(at))

    def st_piece(s, at, a, b):
        lc = st_place(s, at)
        return T.win[:, lc + a:lc + b]

    def cut(s, a, b):
        return (SQ - b, SQ - a) if up(s) else (a, b)

    def hasty(s):
        d = chip_near(s)[0]
        a, b = stream_range(d, *ucols(d, U[0], U[1]))
        return a <= SQ * s and SQ * (s + 1) <= b

    if r < NR - 1:
        A.dma_start(T.fo[:], T.fl[:]).then_inc(S.fo, 16)
    Y.dma_start(T.fls[:], T.fl[:]).then_inc(S.fl, 16)
    regions = []
    own = st_place(r, r)
    Y.dma_start(T.win[:, own:own + SQ], T.st[:]).then_inc(S.st, 16)
    regions.append((own, own + SQ, S.st, 16))

    def load_x(k):
        p, (a, b) = x_place(k), ucols(r, X[k], X[k + 1])
        Y.dma_start(T.win[:, p:p + b - a], T.x[:, a:b]).then_inc(S["x%d" % k], 16)
        regions.append((p, p + b - a, S["x%d" % k], 16))

    for k in range(EARLY):
        load_x(k)

    g.iota(T.pidx[:, 0:1], [[1, 1]], 0, 1).then_inc(S.k_pid, 1)
    g.iota(T.m16[:], [[0, 8], [1, 16]], 0, -1, allow_small_or_imprecise_dtypes=True).then_inc(S.k_m16, 1)
    if r < NR - 1:
        g.wait_ge(S.fo, 16)
        send([(ds, m, T.fo[:], T.cin[:, 64 * r:64 * r + 64], S.fa) for m, ds in flag_groups(r)])

    def piece(s, d, a, b, mask, sem):
        return [d], mask, st_piece(s, r, a, b), st_piece(s, d, a, b), sem

    def arrives(s, a, b, sem, n):
        p = st_place(s, r)
        regions.append((p + a, p + b, sem, n))

    first, middle, last, rest = (0, D[1]), (D[1], D[2]), (D[2], D[3]), (0, D[2])
    g.wait_ge(S.st, 16)
    if r == inner:
        mf, mo = bulk_mask(r, far), bulk_mask(r, on)
        send([piece(r, far, *cut(r, *first), mf, S.f1), piece(r, on, *cut(r, *last), mo, S.aQ)])
        if hasty(r):
            send([piece(r, on, *cut(r, *rest), all_mask(r, on), S.o1)])
            send([piece(r, far, *cut(r, *middle), mf, S.f2)])
        else:
            send([piece(r, far, *cut(r, *middle), mf, S.f2), piece(r, on, *cut(r, *middle), mo, S.o1)])
            send([piece(r, on, *cut(r, *first), all_mask(r, on), S.o1)])
        arrives(far, *cut(far, *first), S.f1, engines(bulk_mask(far, r)))
        arrives(far, *cut(far, *middle), S.f2, engines(bulk_mask(far, r)))
        arrives(far, *cut(far, *last), S.aQ, engines(all_mask(chip_near(far)[0], r)))
        arrives(on, 0, SQ, S.o1, engines(all_mask(on, r)))
    else:
        send([piece(r, on, 0, SQ, all_mask(r, on), S.o1)])
        n = engines(bulk_mask(on, r))
        g.wait_ge(S.aQ, n)
        send([piece(on, far, *cut(on, *last), all_mask(r, far), S.aQ)])
        arrives(on, *cut(on, *last), S.aQ, n)
        arrives(on, *cut(on, *rest), S.o1, engines(all_mask(on, r)) + (0 if hasty(on) else n))
    g.sem_inc(S.go, 1)
    Y.wait_ge(S.go, 1)
    for k in range(EARLY, NX):
        load_x(k)

    blocks = sorted((ucols(r, X[k], X[k + 1]), x_place(k)) for k in range(NX))

    def place(j):
        for (a, b), p in blocks:
            if a <= j < b:
                return p + j - a

    zero = layout(r)[1] - SQ * first_part(r)
    wins = []
    lo = hi = None
    for k in range(NG):
        ja, jb = ucols(r, U[k], U[k + 1])
        sa, sb = stream_range(r, ja, jb)
        ends = [(zero + sa, zero + sb)]
        for (a, b), p in blocks:
            if max(a, ja) < min(b, jb):
                ends.append((p + max(a, ja) - a, p + min(b, jb) - a))
        lo = min([e[0] for e in ends] + ([lo] if k else []))
        hi = max([e[1] for e in ends] + ([hi] if k else []))
        touched = [(p, e) for p, e, sem, n in regions if max(p, lo) < min(e, hi)]
        lo, hi = min(p for p, e in touched), max(e for p, e in touched)
        wins.append((lo, hi))

    cnt = [0]

    def inc(ins):
        name = "v%d" % cnt[0]
        cnt[0] += 1
        ins.then_inc(S[name], 1)
        return S[name]

    s_c16 = []
    at = 0
    for j in [a for (a, b), p in blocks if a > 0 and place(a) != place(a - 16) + 16] + [W]:
        s_c16.append(inc(V.memset(T.c16[:, at:j // 16], 16.0)))
        if j < W:
            s_c16.append(inc(V.memset(T.c16[:, j // 16:j // 16 + 1], float(place(j) - place(j - 16)))))
        at = j // 16 + 1
    s_one = inc(V.memset(T.one[:], 1.0))
    s_onef = inc(V.memset(T.onef[:], 1.0)) if r > 0 else None
    V.wait_ge(S.k_pid, 1)
    s = inc(V.tensor_scalar(T.pand[:, 0:1], T.pidx[:, 0:1], 15, None, Op.bitwise_and))
    V.wait_ge(S.k_m16, 1)
    s_sel = inc(V.tensor_scalar(T.sel[:], T.m16[:], 0.0, None, Op.is_equal))
    s_tri = inc(V.tensor_scalar(T.tri[:], T.m16[:], 0.0, -1.0, Op.is_le, Op.mult))
    V.wait_ge(s, 1)
    s = inc(V.tensor_scalar(T.acol[:, 0:1], T.pand[:, 0:1], float(place(0)), None, Op.add))
    V.wait_ge(s, 1)
    for q in s_c16:
        V.wait_ge(q, 1)
    s_j1 = inc(V.tensor_tensor_scan(T.j1[:], T.c16[:], T.c16[:], T.acol[:, 0:1], Op.add, Op.max))
    V.wait_ge(S.fl, 16)
    s_fb = inc(V.tensor_copy(T.fb[:], T.fls[:]))
    V.wait_ge(s_fb, 1)
    s_rs = inc(V.tensor_tensor_scan(T.rs[:], T.fb[:], T.fb[:], 0.0, Op.add, Op.max))

    A.wait_ge(s_j1, 1)
    A.activation(T.jm[:], T.j1[:], Act.Copy, bias=float(-(16 + zero))).then_inc(S.s_jm, 1)

    chunks = [[0], list(range(1, NG))]

    def span(ks):
        cols = [ucols(r, U[k], U[k + 1]) for k in ks]
        return min(a for a, b in cols) // 16, max(b for a, b in cols) // 16

    for q in (s_sel, s_fb, s_one, s_rs, s_tri):
        E.wait_ge(q, 1)
    for h in (0, 1):
        a, b = span(chunks[h])
        F, P = T["psF%d" % h], T["psP%d" % h]
        E.matmul(F[:, a:b], T.sel[:], T.fb[:, a:b], True, True)
        E.matmul(P[:, a:b], T.one[:], T.rs[:, a:b], True, False)
        E.matmul(P[:, a:b], T.tri[:], T.fb[:, a:b], False, True).then_inc(S["t_l%d" % h], 1)

    def before_c(h):
        a, b = span(chunks[h])
        V.wait_ge(S["t_l%d" % h], 1)
        if h == 0:
            V.wait_ge(S.s_jm, 1)
            V.wait_ge(s_j1, 1)
        s = inc(V.tensor_tensor(T.dd[:, a:b], T["psP%d" % h][:, a:b], T.jm[:, a:b], Op.subtract))
        V.wait_ge(s, 1)
        s = inc(V.tensor_tensor(T.psD[:, a:b], T.dd[:, a:b], T["psF%d" % h][:, a:b], Op.mult))
        V.wait_ge(s, 1)
        s = inc(V.tensor_tensor(T.qq[:, a:b], T.psD[:, a:b], T.j1[:, a:b], Op.add))
        V.wait_ge(s, 1)

    offs = {}

    def after_c(h):
        src = T.qq
        if r > 0:
            a, b = span(chunks[h])
            s = inc(V.tensor_scalar(T.psT[:, a:b], T["psF%d" % h][:, a:b], T.psC[:, 0:1], None, Op.mult))
            V.wait_ge(s, 1)
            s = inc(V.tensor_tensor(T.t2[:, a:b], T.psT[:, a:b], T.qq[:, a:b], Op.add))
            V.wait_ge(s, 1)
            src = T.t2
        ks = chunks[h]
        while ks:
            same = [k for k in ks if wins[k][0] == wins[ks[0]][0]]
            a, b = span(same)
            t = T["off%d" % same[0]]
            q = inc(V.tensor_scalar(t[:, 0:b - a], src[:, a:b], float(16 + wins[same[0]][0]), None, Op.subtract))
            for k in same:
                offs[k] = (q, t, a)
            ks = ks[len(same):]

    before_c(0)
    if r == 0:
        after_c(0)
        before_c(1)
        after_c(1)
    else:
        before_c(1)
        fa = 0
        for q in range(r):
            for m, ds in flag_groups(q):
                if r in ds:
                    fa += engines(m)
        V.wait_ge(S.fa, fa)
        s = inc(V.tensor_copy(T.cf[:, 0:64 * r], T.cin[:, 0:64 * r]))
        V.wait_ge(s, 1)
        s = inc(V.tensor_reduce(T.cs[:, 0:1], T.cf[:, 0:64 * r], AxisListType.X, Op.add))
        E.wait_ge(s, 1)
        E.wait_ge(s_onef, 1)
        E.matmul(T.psC[:, 0:1], T.onef[:], T.cs[:, 0:1], True, True).then_inc(S.t_c, 1)
        V.wait_ge(S.t_c, 1)
        after_c(0)
        after_c(1)

    there = []
    for k in range(NG):
        lo, hi = wins[k]
        new = [(p, sem, n) for p, e, sem, n in regions if max(p, lo) < min(e, hi) and p not in there]
        there += [p for p, sem, n in new]
        s_off, t, c0 = offs[k]
        ja, jb = ucols(r, U[k], U[k + 1])
        jm = ja + (jb - ja) // 64 * 32
        for q in (V, A):
            q.wait_ge(s_off, 1)
            for p, sem, n in new:
                q.wait_ge(sem, n)
        V.tensor_copy(T.yb[:, ja:jm], T.win[:, lo:hi].indirect(t[:, ja // 16 - c0:jm // 16 - c0])
                      ).then_inc(S["vg%d" % k], 1)
        A.activation(T.yb[:, jm:jb], T.win[:, lo:hi].indirect(t[:, jm // 16 - c0:jb // 16 - c0]), Act.Copy
                     ).then_inc(S["sg%d" % k], 1)

    for k in range(NG):
        ja, jb = ucols(r, U[k], U[k + 1])
        Y.wait_ge(S["vg%d" % k], 1)
        Y.wait_ge(S["sg%d" % k], 1)
        Y.dma_start(T.y[:, ja:jb], T.yb[:, ja:jb]).then_inc(S.yst, 16)
    Y.wait_ge(S.yst, 16 * NG)
    g.wait_ge(S.sent, sent[0])
